import numpy as np
import ml_dtypes


def mxq(x, axis, fmt="e4m3"):
    dtype, down = {"e4m3": (ml_dtypes.float8_e4m3fn, 7), "e5m2": (ml_dtypes.float8_e5m2, 14)}[fmt]
    v = np.moveaxis(np.asarray(x, np.float32).astype(ml_dtypes.bfloat16).astype(np.float64), axis, -1)
    blocks = v.reshape(v.shape[:-1] + (-1, 32))
    amax = np.abs(blocks).max(-1, keepdims=True)
    byte = np.maximum(np.where(amax > 0, np.frexp(amax)[1] - 1 + 127, 0) - down, 1)
    scale = np.exp2(byte - 127.0)
    codes = (blocks / scale).astype(np.float32).astype(dtype).astype(np.float64)
    return np.moveaxis((codes * scale).reshape(v.shape), -1, axis)


WIDE = False


def mx_kscale(k):
    if not WIDE:
        return np.ones(k)
    levels = np.array([10, -10, 5, -5, 0])
    if k % 512:
        return np.exp2(np.random.permutation(np.resize(levels, k // 32))).repeat(32)
    a = np.empty((k // 512, 16))
    for p in range(k // 512):
        a[p, :8] = np.random.permutation(np.resize(levels, 8))
        for g in range(8):
            far = levels[np.abs(levels - a[p, g]) >= 10]
            a[p, g + 8] = far[np.random.randint(len(far))]
    return np.exp2(a.ravel()).repeat(32)


def f64(x):
    return np.asarray(x).astype(np.float64)


def striped(idx):
    return np.tile(idx.reshape(-1, 16).T, (8, 1)).astype(np.uint16)


def unstriped(offs):
    return offs[:16].T.reshape(-1).astype(np.int64)


def pack_weight(w):
    k, n = w.shape
    w = f64(np.asarray(w, np.float32).astype(ml_dtypes.bfloat16)).reshape(k // 32, 32, n)
    amax = np.abs(w).max(1)
    byte = np.clip(np.where(amax > 0, np.frexp(amax)[1] - 1 + 127 - 7, 1), 1, 254)
    scaled = (w * np.exp2(127.0 - byte)[:, None, :]).reshape(k, n).astype(np.float32)
    words = np.ascontiguousarray(scaled.reshape(k // 512, 128, 4, n).transpose(0, 1, 3, 2)).astype(ml_dtypes.float8_e4m3fn).view(np.uint8)
    return words, np.ascontiguousarray(byte.astype(np.uint8).reshape(k // 512, 16, n))


def unpack_weight(words, scales):
    g, p, n, _ = words.shape
    vals = np.ascontiguousarray(words).view(ml_dtypes.float8_e4m3fn).astype(np.float64) * np.repeat(np.exp2(scales.astype(np.float64) - 127.0), 8, axis=1)[..., None]
    return vals.transpose(0, 1, 3, 2).reshape(g * 512, n)


def sigmoid(v):
    return 1.0 / (1.0 + np.exp(-np.maximum(v, -700.0)))


K, T, S, D, H, V, Z, W = 512, 2048, 512, 2, 512, 256, 512, 2048
P = 2 ** 7


def setup_inputs():
    n = np.random.standard_normal
    s = mx_kscale(K)[:, None]
    packed_xT = pack_weight(n((K, T)) * s)
    packed_eT = pack_weight(n((K, W)) * s)
    return {
        "x_words": packed_xT[0],
        "x_scales": packed_xT[1],
        "w1": (n((K, H)) / np.sqrt(K) / s).astype(np.float32),
        "w2": (n((K, H)) / np.sqrt(K) / s).astype(np.float32),
        "e_words": packed_eT[0],
        "e_scales": packed_eT[1],
        "unit": (np.random.uniform(0.6, 1.4, (K, 1)) / np.sqrt(K) / s).astype(np.float32),
        "age": (np.tile(np.random.uniform(0.1, 1.5, W), (P, 1))).astype(np.float32),
        "offs": striped(np.random.permutation(T)[:S]),
        "prv": striped(np.random.permutation(S)),
        "art": striped(np.random.permutation(W)[:Z]),
        "mt": striped(np.random.permutation(V)),
        "dup": striped(np.random.permutation(Z)),
    }


def reference(x_words, x_scales, w1, w2, e_words, e_scales, unit, age, offs, prv, art, mt, dup):
    xq = unpack_weight(x_words, x_scales)[:, unstriped(offs)]
    y = mxq(f64(w1), 0, "e4m3").T @ xq
    yp = y[:, unstriped(prv)]
    nov = y - (0.5 * yp)
    yt = mxq(f64(w2), 0, "e4m3").T @ xq
    dw = nov * sigmoid(yt)
    int_ = dw.reshape(len(dw), -1, D).sum(axis=2)
    soc = np.maximum(int_, 0.8 * int_[:, unstriped(mt)])
    hid = f64(unit) * soc
    e_art = unpack_weight(e_words, e_scales)[:, unstriped(art)]
    sc = mxq(hid, 0, "e4m3").T @ e_art
    fr = sc * (np.exp(-1.0 * (f64(age)[:1][:, unstriped(art)])))
    fdd = np.abs(fr - fr[:, unstriped(dup)])
    return np.tanh(fr) + 0.6 * fdd

@@ -1,0 +1,210 @@
+from contextlib import ExitStack
+
+import concourse.mybir as mybir
+
+K, T, S, H, V, Z, W = 512, 2048, 512, 512, 256, 512, 2048
+FLOPS = 2 * K * H * S * 2 + 2 * H * V * Z
+
+F32 = mybir.dt.float32
+BF16 = mybir.dt.bfloat16
+I32 = mybir.dt.int32
+U32 = mybir.dt.uint32
+U16 = mybir.dt.uint16
+U8 = mybir.dt.uint8
+FP8X4 = mybir.dt.float8_e4m3fn_x4
+ALU = mybir.AluOpType
+ACT = mybir.ActivationFunctionType
+
+P = 128
+PACK = 4
+W1_VECTOR_M = 84
+
+
+def tile_picked_ynewsfd_mix_p_kernel(
+    tc, x_words, x_scales, w1, w2, e_words, e_scales, unit, age, offs, prv, art, mt, dup, out
+):
+    nc = tc.nc
+    with ExitStack() as ctx:
+        keep = ctx.enter_context(tc.tile_pool(name="keep", bufs=1))
+        psum = ctx.enter_context(tc.psum_pool(name="psum", bufs=1))
+
+        def sb(name, shape, dtype, tag=None):
+            return keep.tile(shape, dtype, name=name, tag=tag or name, align_bytes=64)
+
+        def load_list(name, src):
+            tile = sb(name, list(src.shape), U16)
+            nc.sync.dma_start(tile[:], src)
+            return tile
+
+        def halves(lst):
+            n = lst.shape[1] // 2
+            return [(slice(16 * n * a, 16 * n * (a + 1)), lst[:, n * a : n * (a + 1)]) for a in range(2)]
+
+        def load_scales(name, src, clearing):
+            tile = sb(name, [P, T], U8)
+            clearing.memset(tile[:].bitcast(I32), 0)
+            for q in range(4):
+                nc.sync.dma_start(tile[32 * q : 32 * q + 4, :].bitcast(I32), src[0, 4 * q : 4 * q + 4, :].bitcast(I32))
+            return tile
+
+        def load_words(name, src):
+            tile = sb(name, [P, T], I32)
+            nc.sync.dma_start(tile[:], src[0].rearrange("p n t -> p (n t)").bitcast(I32))
+            return tile
+
+        w1_raw = sb("w1_raw", [P, PACK, H], F32)
+        nc.sync.dma_start(w1_raw[:], w1.rearrange("(p j) c -> p j c", j=PACK))
+        offs_sb = load_list("offs_sb", offs)
+        prv_sb = load_list("prv_sb", prv)
+        xs_all = load_scales("xs_all", x_scales, nc.gpsimd)
+        xw_all = load_words("xw_all", x_words)
+        w2_raw = []
+        for a in range(2):
+            tile = sb("w2_raw%d" % a, [P, 2, H], F32)
+            nc.sync.dma_start(tile[:], w2.rearrange("(p j) c -> p j c", j=PACK)[:, 2 * a : 2 * a + 2, :])
+            w2_raw.append(tile)
+        unit_sb = sb("unit_sb", [P, PACK], F32)
+        nc.sync.dma_start(unit_sb[:], unit.rearrange("(p t) o -> p (t o)", t=PACK))
+        art_sb = load_list("art_sb", art)
+        mt_sb = load_list("mt_sb", mt)
+        es_all = load_scales("es_all", e_scales, nc.vector)
+        ew_all = load_words("ew_all", e_words)
+        age_sb = sb("age_sb", [P, W], F32)
+        nc.sync.dma_start(age_sb[:], age)
+        dup_sb = load_list("dup_sb", dup)
+
+        w1_bf = sb("w1_bf", [P, PACK * H], BF16)
+        w1_dst = w1_bf[:].rearrange("p (t m j) -> p m j t", t=PACK, j=PACK)
+        w1_src = w1_raw[:].rearrange("p j (m t) -> p m j t", t=PACK)
+        nc.scalar.copy(w1_dst[:, W1_VECTOR_M:], w1_src[:, W1_VECTOR_M:])
+        nc.vector.tensor_copy(w1_dst[:, :W1_VECTOR_M], w1_src[:, :W1_VECTOR_M])
+        w1_codes = sb("w1_codes", [P, H], U32)
+        w1_scales = sb("w1_scales", [P, H], U8)
+        xs = sb("xs", [P, S], U8)
+        nc.vector.tensor_copy(xs[:], xs_all[:].indirect(offs_sb[:]))
+        nc.vector.quantize_mx(out=w1_codes[:].bitcast(FP8X4), scales=w1_scales[:], in_=w1_bf[:])
+
+        xw = sb("xw", [P, S], U32)
+        y_ps = [psum.tile([P, S], F32, name="y_ps%d" % t, tag="bank%d" % t) for t in range(PACK)]
+        for cols, part in halves(offs_sb):
+            nc.vector.tensor_copy(xw[:, cols], xw_all[:].bitcast(U32).indirect(part))
+        for t in range(PACK):
+            rows = slice(P * t, P * (t + 1))
+            for cols, part in halves(offs_sb):
+                nc.tensor.matmul_mx(
+                    out=y_ps[t][:, cols], lhsT=w1_codes[:, rows].bitcast(FP8X4), lhsT_scale=w1_scales[:, rows],
+                    rhs=xw[:, cols].bitcast(FP8X4), rhs_scale=xs[:, cols], start=True, stop=True,
+                )
+
+        w2_bf = sb("w2_bf", [P, PACK * H], BF16)
+        w2_dst = w2_bf[:].rearrange("p (t m j) -> p m j t", t=PACK, j=PACK)
+        for a in range(2):
+            nc.vector.tensor_copy(w2_dst[:, :, 2 * a : 2 * a + 2, :], w2_raw[a][:].rearrange("p j (m t) -> p m j t", t=PACK))
+        w2_codes = sb("w2_codes", [P, H], U32)
+        w2_scales = sb("w2_scales", [P, H], U8)
+        yt_ps = [psum.tile([P, S], F32, name="yt_ps%d" % t, tag="bank%d" % (PACK + t)) for t in range(PACK)]
+        for u in range(2):
+            span = slice(2 * P * u, 2 * P * (u + 1))
+            nc.vector.quantize_mx(
+                out=w2_codes[:, span].bitcast(FP8X4), scales=w2_scales[:, span],
+                in_=w2_bf[:, PACK * 2 * P * u : PACK * 2 * P * (u + 1)],
+            )
+            for t in range(2 * u, 2 * u + 2):
+                rows = slice(P * t, P * (t + 1))
+                nc.tensor.matmul_mx(
+                    out=yt_ps[t][:], lhsT=w2_codes[:, rows].bitcast(FP8X4), lhsT_scale=w2_scales[:, rows],
+                    rhs=xw[:].bitcast(FP8X4), rhs_scale=xs[:], start=True, stop=True,
+                )
+
+        half_unit = sb("half_unit", [P, PACK], F32)
+        nc.gpsimd.tensor_scalar(half_unit[:], unit_sb[:], 0.5, 0.0, ALU.mult, ALU.add)
+
+        y_sb = [sb("y_sb%d" % t, [P, S], F32) for t in range(PACK)]
+        yp = [sb("yp%d" % t, [P, S], F32) for t in range(PACK)]
+        th = [sb("th%d" % t, [P, S], F32) for t in range(PACK)]
+        nov = [sb("nov%d" % t, [P, S], F32) for t in range(PACK)]
+        dw = [sb("dw%d" % t, [P, S], F32) for t in range(PACK)]
+        interest = [sb("interest%d" % t, [P, V], F32) for t in range(PACK)]
+        mate = [sb("mate%d" % t, [P, V], F32) for t in range(PACK)]
+        soc = [sb("soc%d" % t, [P, V], F32) for t in range(PACK)]
+        hid_bf = [sb("hid_bf%d" % h, [P, P, PACK], BF16) for h in range(2)]
+
+        def fetch(engine, dst, window, part):
+            if engine == "scalar":
+                nc.scalar.activation(dst, window.indirect(part), ACT.Copy)
+            else:
+                nc.vector.tensor_copy(dst, window.indirect(part))
+
+        def fetch_previous(t):
+            nc.scalar.copy(y_sb[t][:], y_ps[t][:])
+            for a, (cols, part) in enumerate(halves(prv_sb)):
+                fetch("vector" if (t, a) == (0, 1) else "scalar", yp[t][:, cols], y_sb[t][:], part)
+
+        def gate(t):
+            nc.scalar.activation(th[t][:], yt_ps[t][:], ACT.Tanh, scale=0.5)
+
+        def make_interest(t):
+            nc.vector.scalar_tensor_tensor(nov[t][:], yp[t][:], -0.5, y_ps[t][:], ALU.mult, ALU.add)
+            nc.vector.scalar_tensor_tensor(dw[t][:], th[t][:], 1.0, nov[t][:], ALU.add, ALU.mult)
+            nc.vector.tensor_tensor(interest[t][:], dw[t][:, 0::2], dw[t][:, 1::2], ALU.add)
+
+        def compete(t):
+            for h, (cols, part) in enumerate(halves(mt_sb)):
+                fetch("scalar", mate[t][:, cols], interest[t][:], part)
+            pieces = [slice(0, P), slice(P, V)] if t == PACK - 1 else [slice(0, V)]
+            for cols in pieces:
+                nc.vector.scalar_tensor_tensor(soc[t][:, cols], mate[t][:, cols], 0.8, interest[t][:, cols], ALU.mult, ALU.max)
+            for h in range(2):
+                nc.vector.tensor_scalar(hid_bf[h][:, :, t], soc[t][:, P * h : P * (h + 1)], half_unit[:, t : t + 1], None, ALU.mult)
+
+        fetch_previous(0)
+        fetch_previous(1)
+        for t in range(2):
+            gate(t)
+            make_interest(t)
+        for t in range(2, PACK):
+            fetch_previous(t)
+            gate(t)
+            make_interest(t)
+        for t in range(PACK):
+            compete(t)
+
+        es = sb("es", [P, Z], U8, tag="w2_bf")
+        nc.vector.tensor_copy(es[:], es_all[:].indirect(art_sb[:]))
+        ew = sb("ew", [P, Z], U32, tag="dw0")
+        nc.vector.tensor_copy(ew[:], ew_all[:].bitcast(U32).indirect(art_sb[:]))
+        fade = sb("fade", [P, Z], F32, tag="dw3")
+        nc.scalar.activation(fade[:], age_sb[:].indirect(art_sb[:]), ACT.Exp, scale=-1.0)
+
+        hid_codes = sb("hid_codes", [P, V], U32)
+        hid_scales = sb("hid_scales", [P, V], U8)
+        sc_ps = [psum.tile([P, Z], F32, name="sc_ps%d" % h, tag="bank%d" % h) for h in range(2)]
+        fr = [sb("fr%d" % h, [P, Z], F32) for h in range(2)]
+        twin = [sb("twin%d" % h, [P, Z], F32) for h in range(2)]
+        tfr = [sb("tfr%d" % h, [P, Z], F32) for h in range(2)]
+        diff = [sb("diff%d" % h, [P, Z], F32) for h in range(2)]
+        dist = [sb("dist%d" % h, [P, Z], F32) for h in range(2)]
+        res = [sb("res%d" % h, [P, Z], F32) for h in range(2)]
+        for h in range(2):
+            rows = slice(P * h, P * (h + 1))
+            nc.vector.quantize_mx(
+                out=hid_codes[:, rows].bitcast(FP8X4), scales=hid_scales[:, rows],
+                in_=hid_bf[h][:].rearrange("p v t -> p (v t)"),
+            )
+            nc.tensor.matmul_mx(
+                out=sc_ps[h][:], lhsT=hid_codes[:, rows].bitcast(FP8X4), lhsT_scale=hid_scales[:, rows],
+                rhs=ew[:].bitcast(FP8X4), rhs_scale=es[:], start=True, stop=True,
+            )
+        for h in range(2):
+            nc.vector.tensor_tensor(fr[h][:], sc_ps[h][:], fade[:], ALU.mult)
+            for a, (cols, part) in enumerate(halves(dup_sb)):
+                fetch("scalar" if a == 0 else "vector", twin[h][:, cols], fr[h][:], part)
+            nc.scalar.activation(tfr[h][:], fr[h][:], ACT.Tanh)
+        for h in range(2):
+            for cols, part in halves(dup_sb):
+                nc.vector.tensor_tensor(diff[h][:, cols], fr[h][:, cols], twin[h][:, cols], ALU.subtract)
+                nc.scalar.activation(dist[h][:, cols], diff[h][:, cols], ACT.Abs, scale=0.6)
+        for h in range(2):
+            for cols, part in halves(dup_sb):
+                nc.vector.tensor_tensor(res[h][:, cols], dist[h][:, cols], tfr[h][:, cols], ALU.add)
+                nc.sync.dma_start(out[P * h : P * (h + 1), cols], res[h][:, cols])

@@ -40,38 +40,38 @@ def tile_picked_ynewsfd_mix_p_kernel(
             n = lst.shape[1] // 2
             return [(slice(16 * n * a, 16 * n * (a + 1)), lst[:, n * a : n * (a + 1)]) for a in range(2)]
 
-        def load_scales(name, src, clearing):
-            tile = sb(name, [P, T], U8)
-            clearing.memset(tile[:].bitcast(I32), 0)
-            for q in range(4):
-                nc.sync.dma_start(tile[32 * q : 32 * q + 4, :].bitcast(I32), src[0, 4 * q : 4 * q + 4, :].bitcast(I32))
-            return tile
-
         def load_words(name, src):
             tile = sb(name, [P, T], I32)
             nc.sync.dma_start(tile[:], src[0].rearrange("p n t -> p (n t)").bitcast(I32))
+            return tile
+
+        def load_scales(name, src):
+            tile = sb(name, [P, T], U8)
+            nc.vector.memset(tile[:].bitcast(I32), 0)
+            for q in range(4):
+                nc.sync.dma_start(tile[32 * q : 32 * q + 4, :].bitcast(I32), src[0, 4 * q : 4 * q + 4, :].bitcast(I32))
             return tile
 
         w1_raw = sb("w1_raw", [P, PACK, H], F32)
         nc.sync.dma_start(w1_raw[:], w1.rearrange("(p j) c -> p j c", j=PACK))
         offs_sb = load_list("offs_sb", offs)
         prv_sb = load_list("prv_sb", prv)
-        xs_all = load_scales("xs_all", x_scales, nc.gpsimd)
+        xs_all = load_scales("xs_all", x_scales)
         xw_all = load_words("xw_all", x_words)
         w2_raw = []
         for a in range(2):
             tile = sb("w2_raw%d" % a, [P, 2, H], F32)
             nc.sync.dma_start(tile[:], w2.rearrange("(p j) c -> p j c", j=PACK)[:, 2 * a : 2 * a + 2, :])
             w2_raw.append(tile)
+        art_sb = load_list("art_sb", art)
+        es_all = load_scales("es_all", e_scales)
+        ew_all = load_words("ew_all", e_words)
         unit_sb = sb("unit_sb", [P, PACK], F32)
         nc.sync.dma_start(unit_sb[:], unit.rearrange("(p t) o -> p (t o)", t=PACK))
-        art_sb = load_list("art_sb", art)
         mt_sb = load_list("mt_sb", mt)
-        es_all = load_scales("es_all", e_scales, nc.vector)
-        ew_all = load_words("ew_all", e_words)
+        dup_sb = load_list("dup_sb", dup)
         age_sb = sb("age_sb", [P, W], F32)
         nc.sync.dma_start(age_sb[:], age)
-        dup_sb = load_list("dup_sb", dup)
 
         w1_bf = sb("w1_bf", [P, PACK * H], BF16)
         w1_dst = w1_bf[:].rearrange("p (t m j) -> p m j t", t=PACK, j=PACK)
@@ -85,16 +85,21 @@ def tile_picked_ynewsfd_mix_p_kernel(
         nc.vector.quantize_mx(out=w1_codes[:].bitcast(FP8X4), scales=w1_scales[:], in_=w1_bf[:])
 
         xw = sb("xw", [P, S], U32)
-        y_ps = [psum.tile([P, S], F32, name="y_ps%d" % t, tag="bank%d" % t) for t in range(PACK)]
-        for cols, part in halves(offs_sb):
+        y_sb = [sb("y_sb%d" % t, [P, S], F32) for t in range(PACK)]
+
+        def product(name, bank, codes, scales, rows, moving, moving_scales, cols):
+            acc = psum.tile([P, cols.stop - cols.start], F32, name=name, tag="bank%d" % bank)
+            nc.tensor.matmul_mx(
+                out=acc[:], lhsT=codes[:, rows].bitcast(FP8X4), lhsT_scale=scales[:, rows],
+                rhs=moving[:, cols].bitcast(FP8X4), rhs_scale=moving_scales[:, cols], start=True, stop=True,
+            )
+            return acc
+
+        for a, (cols, part) in enumerate(halves(offs_sb)):
             nc.vector.tensor_copy(xw[:, cols], xw_all[:].bitcast(U32).indirect(part))
-        for t in range(PACK):
-            rows = slice(P * t, P * (t + 1))
-            for cols, part in halves(offs_sb):
-                nc.tensor.matmul_mx(
-                    out=y_ps[t][:, cols], lhsT=w1_codes[:, rows].bitcast(FP8X4), lhsT_scale=w1_scales[:, rows],
-                    rhs=xw[:, cols].bitcast(FP8X4), rhs_scale=xs[:, cols], start=True, stop=True,
-                )
+            acc = product("y0_ps%d" % a, 3 * a, w1_codes, w1_scales, slice(0, P), xw, xs, cols)
+            nc.scalar.activation(y_sb[0][:, cols], acc[:], ACT.Copy, scale=0.5)
+        y_ps = {t: product("y_ps%d" % t, t, w1_codes, w1_scales, slice(P * t, P * (t + 1)), xw, xs, slice(0, S)) for t in range(1, PACK - 1)}
 
         w2_bf = sb("w2_bf", [P, PACK * H], BF16)
         w2_dst = w2_bf[:].rearrange("p (t m j) -> p m j t", t=PACK, j=PACK)
@@ -102,31 +107,17 @@ def tile_picked_ynewsfd_mix_p_kernel(
             nc.vector.tensor_copy(w2_dst[:, :, 2 * a : 2 * a + 2, :], w2_raw[a][:].rearrange("p j (m t) -> p m j t", t=PACK))
         w2_codes = sb("w2_codes", [P, H], U32)
         w2_scales = sb("w2_scales", [P, H], U8)
-        yt_ps = [psum.tile([P, S], F32, name="yt_ps%d" % t, tag="bank%d" % (PACK + t)) for t in range(PACK)]
-        for u in range(2):
-            span = slice(2 * P * u, 2 * P * (u + 1))
-            nc.vector.quantize_mx(
-                out=w2_codes[:, span].bitcast(FP8X4), scales=w2_scales[:, span],
-                in_=w2_bf[:, PACK * 2 * P * u : PACK * 2 * P * (u + 1)],
-            )
-            for t in range(2 * u, 2 * u + 2):
-                rows = slice(P * t, P * (t + 1))
-                nc.tensor.matmul_mx(
-                    out=yt_ps[t][:], lhsT=w2_codes[:, rows].bitcast(FP8X4), lhsT_scale=w2_scales[:, rows],
-                    rhs=xw[:].bitcast(FP8X4), rhs_scale=xs[:], start=True, stop=True,
-                )
+        nc.vector.quantize_mx(out=w2_codes[:].bitcast(FP8X4), scales=w2_scales[:], in_=w2_bf[:])
+        yt_ps = [product("yt_ps%d" % t, PACK + t, w2_codes, w2_scales, slice(P * t, P * (t + 1)), xw, xs, slice(0, S)) for t in range(PACK)]
 
-        half_unit = sb("half_unit", [P, PACK], F32)
-        nc.gpsimd.tensor_scalar(half_unit[:], unit_sb[:], 0.5, 0.0, ALU.mult, ALU.add)
-
-        y_sb = [sb("y_sb%d" % t, [P, S], F32) for t in range(PACK)]
-        yp = [sb("yp%d" % t, [P, S], F32) for t in range(PACK)]
+        yp = [sb("yp%d" % t, [P, S], F32, tag="w2_raw1" if t == 0 else None) for t in range(PACK)]
         th = [sb("th%d" % t, [P, S], F32) for t in range(PACK)]
-        nov = [sb("nov%d" % t, [P, S], F32) for t in range(PACK)]
+        nov = {}
         dw = [sb("dw%d" % t, [P, S], F32) for t in range(PACK)]
         interest = [sb("interest%d" % t, [P, V], F32) for t in range(PACK)]
         mate = [sb("mate%d" % t, [P, V], F32) for t in range(PACK)]
         soc = [sb("soc%d" % t, [P, V], F32) for t in range(PACK)]
+        hid_rows = sb("hid_rows", [P, PACK, V], BF16)
         hid_bf = [sb("hid_bf%d" % h, [P, P, PACK], BF16) for h in range(2)]
 
         def fetch(engine, dst, window, part):
@@ -135,50 +126,89 @@ def tile_picked_ynewsfd_mix_p_kernel(
             else:
                 nc.vector.tensor_copy(dst, window.indirect(part))
 
+        def leave_psum(t):
+            nc.scalar.activation(y_sb[t][:, :S], y_ps[t][:], ACT.Copy, scale=0.5)
+
         def fetch_previous(t):
-            nc.scalar.copy(y_sb[t][:], y_ps[t][:])
-            for a, (cols, part) in enumerate(halves(prv_sb)):
-                fetch("vector" if (t, a) == (0, 1) else "scalar", yp[t][:, cols], y_sb[t][:], part)
+            for cols, part in halves(prv_sb):
+                fetch("vector" if t == 0 else "scalar", yp[t][:, cols], y_sb[t][:], part)
 
         def gate(t):
             nc.scalar.activation(th[t][:], yt_ps[t][:], ACT.Tanh, scale=0.5)
 
-        def make_interest(t):
-            nc.vector.scalar_tensor_tensor(nov[t][:], yp[t][:], -0.5, y_ps[t][:], ALU.mult, ALU.add)
+        def novelty(t):
+            nov[t] = sb("nov%d" % t, [P, S], F32, tag=[None, "w2_raw1", "yp1", "yp2"][t])
+            nc.vector.scalar_tensor_tensor(nov[t][:], yp[t][:], -0.5, y_sb[t][:, :S], ALU.mult, ALU.add)
+
+        def gated(t):
             nc.vector.scalar_tensor_tensor(dw[t][:], th[t][:], 1.0, nov[t][:], ALU.add, ALU.mult)
-            nc.vector.tensor_tensor(interest[t][:], dw[t][:, 0::2], dw[t][:, 1::2], ALU.add)
 
-        def compete(t):
-            for h, (cols, part) in enumerate(halves(mt_sb)):
-                fetch("scalar", mate[t][:, cols], interest[t][:], part)
-            pieces = [slice(0, P), slice(P, V)] if t == PACK - 1 else [slice(0, V)]
-            for cols in pieces:
-                nc.vector.scalar_tensor_tensor(soc[t][:, cols], mate[t][:, cols], 0.8, interest[t][:, cols], ALU.mult, ALU.max)
-            for h in range(2):
-                nc.vector.tensor_scalar(hid_bf[h][:, :, t], soc[t][:, P * h : P * (h + 1)], half_unit[:, t : t + 1], None, ALU.mult)
+        def pair_sum(t):
+            nc.vector.tensor_tensor(interest[t][:, :V], dw[t][:, 0::2], dw[t][:, 1::2], ALU.add)
 
+        def compete(t, cols):
+            nc.vector.scalar_tensor_tensor(soc[t][:, cols], mate[t][:, cols], 0.8, interest[t][:, cols], ALU.mult, ALU.max)
+
+        leave_psum(1)
         fetch_previous(0)
         fetch_previous(1)
-        for t in range(2):
-            gate(t)
-            make_interest(t)
-        for t in range(2, PACK):
-            fetch_previous(t)
-            gate(t)
-            make_interest(t)
-        for t in range(PACK):
-            compete(t)
-
+        leave_psum(2)
+        fetch_previous(2)
+        gate(0)
+        gate(1)
+        y_ps[3] = product("y_ps3", PACK, w1_codes, w1_scales, slice(P * 3, P * 4), xw, xs, slice(0, S))
+        leave_psum(3)
+        fetch_previous(3)
+        gate(2)
+        gate(3)
         es = sb("es", [P, Z], U8, tag="w2_bf")
         nc.vector.tensor_copy(es[:], es_all[:].indirect(art_sb[:]))
-        ew = sb("ew", [P, Z], U32, tag="dw0")
+        novelty(0)
+        ew = sb("ew", [P, Z], U32, tag="w2_raw0")
         nc.vector.tensor_copy(ew[:], ew_all[:].bitcast(U32).indirect(art_sb[:]))
-        fade = sb("fade", [P, Z], F32, tag="dw3")
+        novelty(1)
+        novelty(2)
+        for u in range(2):
+            gated(2 * u)
+            gated(2 * u + 1)
+            pair_sum(2 * u)
+            pair_sum(2 * u + 1)
+            if u == 0:
+                novelty(3)
+        last = PACK - 1
+        for t in range(PACK):
+            for cols, part in halves(mt_sb):
+                fetch("scalar", mate[t][:, cols], interest[t][:], part)
+        for t in range(last):
+            compete(t, slice(0, V))
+            if t < last - 1:
+                nc.vector.tensor_scalar(hid_rows[:, t, :], soc[t][:], unit_sb[:, t : t + 1], None, ALU.mult)
+            else:
+                nc.scalar.activation(hid_rows[:, t, :], soc[t][:], ACT.Copy, scale=unit_sb[:, t : t + 1])
+
+        hid_codes = [sb("hid_codes%d" % h, [P, P], U32) for h in range(2)]
+        hid_scales = [sb("hid_scales%d" % h, [P, P], U8) for h in range(2)]
+        sc_ps = {}
+        for h in range(2):
+            rows = slice(P * h, P * (h + 1))
+            compete(last, rows)
+            nc.vector.tensor_scalar(hid_rows[:, last, rows], soc[last][:, rows], unit_sb[:, last : last + 1], None, ALU.mult)
+        for h in range(2):
+            rows = slice(P * h, P * (h + 1))
+            nc.vector.tensor_copy(
+                hid_bf[h][:].rearrange("p (c i) t -> p c t i", i=4),
+                hid_rows[:, :, rows].rearrange("p t (c i) -> p c t i", i=4),
+            )
+            nc.vector.quantize_mx(
+                out=hid_codes[h][:].bitcast(FP8X4), scales=hid_scales[h][:],
+                in_=hid_bf[h][:].rearrange("p v t -> p (v t)"),
+            )
+            for a, (cols, part) in enumerate(halves(art_sb)):
+                sc_ps[h, a] = product("sc_ps%d%d" % (h, a), 2 * h + a, hid_codes[h], hid_scales[h], slice(0, P), ew, es, cols)
+
+        fade = sb("fade", [P, Z], F32, tag="interest3")
         nc.scalar.activation(fade[:], age_sb[:].indirect(art_sb[:]), ACT.Exp, scale=-1.0)
 
-        hid_codes = sb("hid_codes", [P, V], U32)
-        hid_scales = sb("hid_scales", [P, V], U8)
-        sc_ps = [psum.tile([P, Z], F32, name="sc_ps%d" % h, tag="bank%d" % h) for h in range(2)]
         fr = [sb("fr%d" % h, [P, Z], F32) for h in range(2)]
         twin = [sb("twin%d" % h, [P, Z], F32) for h in range(2)]
         tfr = [sb("tfr%d" % h, [P, Z], F32) for h in range(2)]
@@ -186,25 +216,17 @@ def tile_picked_ynewsfd_mix_p_kernel(
         dist = [sb("dist%d" % h, [P, Z], F32) for h in range(2)]
         res = [sb("res%d" % h, [P, Z], F32) for h in range(2)]
         for h in range(2):
-            rows = slice(P * h, P * (h + 1))
-            nc.vector.quantize_mx(
-                out=hid_codes[:, rows].bitcast(FP8X4), scales=hid_scales[:, rows],
-                in_=hid_bf[h][:].rearrange("p v t -> p (v t)"),
-            )
-            nc.tensor.matmul_mx(
-                out=sc_ps[h][:], lhsT=hid_codes[:, rows].bitcast(FP8X4), lhsT_scale=hid_scales[:, rows],
-                rhs=ew[:].bitcast(FP8X4), rhs_scale=es[:], start=True, stop=True,
-            )
-        for h in range(2):
-            nc.vector.tensor_tensor(fr[h][:], sc_ps[h][:], fade[:], ALU.mult)
+            for a, (cols, part) in enumerate(halves(art_sb)):
+                nc.vector.tensor_tensor(fr[h][:, cols], sc_ps[h, a][:], fade[:, cols], ALU.mult)
             for a, (cols, part) in enumerate(halves(dup_sb)):
                 fetch("scalar" if a == 0 else "vector", twin[h][:, cols], fr[h][:], part)
-            nc.scalar.activation(tfr[h][:], fr[h][:], ACT.Tanh)
+            for cols, part in halves(dup_sb):
+                nc.scalar.activation(tfr[h][:, cols], fr[h][:, cols], ACT.Tanh)
         for h in range(2):
             for cols, part in halves(dup_sb):
                 nc.vector.tensor_tensor(diff[h][:, cols], fr[h][:, cols], twin[h][:, cols], ALU.subtract)
+            for cols, part in halves(dup_sb):
                 nc.scalar.activation(dist[h][:, cols], diff[h][:, cols], ACT.Abs, scale=0.6)
-        for h in range(2):
             for cols, part in halves(dup_sb):
                 nc.vector.tensor_tensor(res[h][:, cols], dist[h][:, cols], tfr[h][:, cols], ALU.add)
                 nc.sync.dma_start(out[P * h : P * (h + 1), cols], res[h][:, cols])

from contextlib import ExitStack

import concourse.mybir as mybir

K, T, S, H, V, Z, W = 512, 2048, 512, 512, 256, 512, 2048
FLOPS = 2 * K * H * S * 2 + 2 * H * V * Z

F32 = mybir.dt.float32
BF16 = mybir.dt.bfloat16
I32 = mybir.dt.int32
U32 = mybir.dt.uint32
U16 = mybir.dt.uint16
U8 = mybir.dt.uint8
FP8X4 = mybir.dt.float8_e4m3fn_x4
ALU = mybir.AluOpType
ACT = mybir.ActivationFunctionType

P = 128
PACK = 4
W1_VECTOR_M = 84


def tile_picked_ynewsfd_mix_p_kernel(
    tc, x_words, x_scales, w1, w2, e_words, e_scales, unit, age, offs, prv, art, mt, dup, out
):
    nc = tc.nc
    with ExitStack() as ctx:
        keep = ctx.enter_context(tc.tile_pool(name="keep", bufs=1))
        psum = ctx.enter_context(tc.psum_pool(name="psum", bufs=1))

        def sb(name, shape, dtype, tag=None):
            return keep.tile(shape, dtype, name=name, tag=tag or name, align_bytes=64)

        def load_list(name, src):
            tile = sb(name, list(src.shape), U16)
            nc.sync.dma_start(tile[:], src)
            return tile

        def halves(lst):
            n = lst.shape[1] // 2
            return [(slice(16 * n * a, 16 * n * (a + 1)), lst[:, n * a : n * (a + 1)]) for a in range(2)]

        def load_words(name, src):
            tile = sb(name, [P, T], I32)
            nc.sync.dma_start(tile[:], src[0].rearrange("p n t -> p (n t)").bitcast(I32))
            return tile

        def load_scales(name, src):
            tile = sb(name, [P, T], U8)
            nc.vector.memset(tile[:].bitcast(I32), 0)
            for q in range(4):
                nc.sync.dma_start(tile[32 * q : 32 * q + 4, :].bitcast(I32), src[0, 4 * q : 4 * q + 4, :].bitcast(I32))
            return tile

        w1_raw = sb("w1_raw", [P, PACK, H], F32)
        nc.sync.dma_start(w1_raw[:], w1.rearrange("(p j) c -> p j c", j=PACK))
        offs_sb = load_list("offs_sb", offs)
        prv_sb = load_list("prv_sb", prv)
        xs_all = load_scales("xs_all", x_scales)
        xw_all = load_words("xw_all", x_words)
        w2_raw = []
        for a in range(2):
            tile = sb("w2_raw%d" % a, [P, 2, H], F32)
            nc.sync.dma_start(tile[:], w2.rearrange("(p j) c -> p j c", j=PACK)[:, 2 * a : 2 * a + 2, :])
            w2_raw.append(tile)
        art_sb = load_list("art_sb", art)
        es_all = load_scales("es_all", e_scales)
        ew_all = load_words("ew_all", e_words)
        unit_sb = sb("unit_sb", [P, PACK], F32)
        nc.sync.dma_start(unit_sb[:], unit.rearrange("(p t) o -> p (t o)", t=PACK))
        mt_sb = load_list("mt_sb", mt)
        dup_sb = load_list("dup_sb", dup)
        age_sb = sb("age_sb", [P, W], F32)
        nc.sync.dma_start(age_sb[:], age)

        w1_bf = sb("w1_bf", [P, PACK * H], BF16)
        w1_dst = w1_bf[:].rearrange("p (t m j) -> p m j t", t=PACK, j=PACK)
        w1_src = w1_raw[:].rearrange("p j (m t) -> p m j t", t=PACK)
        nc.scalar.copy(w1_dst[:, W1_VECTOR_M:], w1_src[:, W1_VECTOR_M:])
        nc.vector.tensor_copy(w1_dst[:, :W1_VECTOR_M], w1_src[:, :W1_VECTOR_M])
        w1_codes = sb("w1_codes", [P, H], U32)
        w1_scales = sb("w1_scales", [P, H], U8)
        xs = sb("xs", [P, S], U8)
        nc.vector.tensor_copy(xs[:], xs_all[:].indirect(offs_sb[:]))
        nc.vector.quantize_mx(out=w1_codes[:].bitcast(FP8X4), scales=w1_scales[:], in_=w1_bf[:])

        xw = sb("xw", [P, S], U32)
        y_sb = [sb("y_sb%d" % t, [P, S], F32) for t in range(PACK)]

        def product(name, bank, codes, scales, rows, moving, moving_scales, cols):
            acc = psum.tile([P, cols.stop - cols.start], F32, name=name, tag="bank%d" % bank)
            nc.tensor.matmul_mx(
                out=acc[:], lhsT=codes[:, rows].bitcast(FP8X4), lhsT_scale=scales[:, rows],
                rhs=moving[:, cols].bitcast(FP8X4), rhs_scale=moving_scales[:, cols], start=True, stop=True,
            )
            return acc

        for a, (cols, part) in enumerate(halves(offs_sb)):
            nc.vector.tensor_copy(xw[:, cols], xw_all[:].bitcast(U32).indirect(part))
            acc = product("y0_ps%d" % a, 3 * a, w1_codes, w1_scales, slice(0, P), xw, xs, cols)
            nc.scalar.activation(y_sb[0][:, cols], acc[:], ACT.Copy, scale=0.5)
        y_ps = {t: product("y_ps%d" % t, t, w1_codes, w1_scales, slice(P * t, P * (t + 1)), xw, xs, slice(0, S)) for t in range(1, PACK - 1)}

        w2_bf = sb("w2_bf", [P, PACK * H], BF16)
        w2_dst = w2_bf[:].rearrange("p (t m j) -> p m j t", t=PACK, j=PACK)
        for a in range(2):
            nc.vector.tensor_copy(w2_dst[:, :, 2 * a : 2 * a + 2, :], w2_raw[a][:].rearrange("p j (m t) -> p m j t", t=PACK))
        w2_codes = sb("w2_codes", [P, H], U32)
        w2_scales = sb("w2_scales", [P, H], U8)
        nc.vector.quantize_mx(out=w2_codes[:].bitcast(FP8X4), scales=w2_scales[:], in_=w2_bf[:])
        yt_ps = [product("yt_ps%d" % t, PACK + t, w2_codes, w2_scales, slice(P * t, P * (t + 1)), xw, xs, slice(0, S)) for t in range(PACK)]

        yp = [sb("yp%d" % t, [P, S], F32, tag="w2_raw1" if t == 0 else None) for t in range(PACK)]
        th = [sb("th%d" % t, [P, S], F32) for t in range(PACK)]
        nov = {}
        dw = [sb("dw%d" % t, [P, S], F32) for t in range(PACK)]
        interest = [sb("interest%d" % t, [P, V], F32) for t in range(PACK)]
        mate = [sb("mate%d" % t, [P, V], F32) for t in range(PACK)]
        soc = [sb("soc%d" % t, [P, V], F32) for t in range(PACK)]
        hid_rows = sb("hid_rows", [P, PACK, V], BF16)
        hid_bf = [sb("hid_bf%d" % h, [P, P, PACK], BF16) for h in range(2)]

        def fetch(engine, dst, window, part):
            if engine == "scalar":
                nc.scalar.activation(dst, window.indirect(part), ACT.Copy)
            else:
                nc.vector.tensor_copy(dst, window.indirect(part))

        def leave_psum(t):
            nc.scalar.activation(y_sb[t][:, :S], y_ps[t][:], ACT.Copy, scale=0.5)

        def fetch_previous(t):
            for cols, part in halves(prv_sb):
                fetch("vector" if t == 0 else "scalar", yp[t][:, cols], y_sb[t][:], part)

        def gate(t):
            nc.scalar.activation(th[t][:], yt_ps[t][:], ACT.Tanh, scale=0.5)

        def novelty(t):
            nov[t] = sb("nov%d" % t, [P, S], F32, tag=[None, "w2_raw1", "yp1", "yp2"][t])
            nc.vector.scalar_tensor_tensor(nov[t][:], yp[t][:], -0.5, y_sb[t][:, :S], ALU.mult, ALU.add)

        def gated(t):
            nc.vector.scalar_tensor_tensor(dw[t][:], th[t][:], 1.0, nov[t][:], ALU.add, ALU.mult)

        def pair_sum(t):
            nc.vector.tensor_tensor(interest[t][:, :V], dw[t][:, 0::2], dw[t][:, 1::2], ALU.add)

        def compete(t, cols):
            nc.vector.scalar_tensor_tensor(soc[t][:, cols], mate[t][:, cols], 0.8, interest[t][:, cols], ALU.mult, ALU.max)

        leave_psum(1)
        fetch_previous(0)
        fetch_previous(1)
        leave_psum(2)
        fetch_previous(2)
        gate(0)
        gate(1)
        y_ps[3] = product("y_ps3", PACK, w1_codes, w1_scales, slice(P * 3, P * 4), xw, xs, slice(0, S))
        leave_psum(3)
        fetch_previous(3)
        gate(2)
        gate(3)
        es = sb("es", [P, Z], U8, tag="w2_bf")
        nc.vector.tensor_copy(es[:], es_all[:].indirect(art_sb[:]))
        novelty(0)
        ew = sb("ew", [P, Z], U32, tag="w2_raw0")
        nc.vector.tensor_copy(ew[:], ew_all[:].bitcast(U32).indirect(art_sb[:]))
        novelty(1)
        novelty(2)
        for u in range(2):
            gated(2 * u)
            gated(2 * u + 1)
            pair_sum(2 * u)
            pair_sum(2 * u + 1)
            if u == 0:
                novelty(3)
        last = PACK - 1
        for t in range(PACK):
            for cols, part in halves(mt_sb):
                fetch("scalar", mate[t][:, cols], interest[t][:], part)
        for t in range(last):
            compete(t, slice(0, V))
            if t < last - 1:
                nc.vector.tensor_scalar(hid_rows[:, t, :], soc[t][:], unit_sb[:, t : t + 1], None, ALU.mult)
            else:
                nc.scalar.activation(hid_rows[:, t, :], soc[t][:], ACT.Copy, scale=unit_sb[:, t : t + 1])

        hid_codes = [sb("hid_codes%d" % h, [P, P], U32) for h in range(2)]
        hid_scales = [sb("hid_scales%d" % h, [P, P], U8) for h in range(2)]
        sc_ps = {}
        for h in range(2):
            rows = slice(P * h, P * (h + 1))
            compete(last, rows)
            nc.vector.tensor_scalar(hid_rows[:, last, rows], soc[last][:, rows], unit_sb[:, last : last + 1], None, ALU.mult)
        for h in range(2):
            rows = slice(P * h, P * (h + 1))
            nc.vector.tensor_copy(
                hid_bf[h][:].rearrange("p (c i) t -> p c t i", i=4),
                hid_rows[:, :, rows].rearrange("p t (c i) -> p c t i", i=4),
            )
            nc.vector.quantize_mx(
                out=hid_codes[h][:].bitcast(FP8X4), scales=hid_scales[h][:],
                in_=hid_bf[h][:].rearrange("p v t -> p (v t)"),
            )
            for a, (cols, part) in enumerate(halves(art_sb)):
                sc_ps[h, a] = product("sc_ps%d%d" % (h, a), 2 * h + a, hid_codes[h], hid_scales[h], slice(0, P), ew, es, cols)

        fade = sb("fade", [P, Z], F32, tag="interest3")
        nc.scalar.activation(fade[:], age_sb[:].indirect(art_sb[:]), ACT.Exp, scale=-1.0)

        fr = [sb("fr%d" % h, [P, Z], F32) for h in range(2)]
        twin = [sb("twin%d" % h, [P, Z], F32) for h in range(2)]
        tfr = [sb("tfr%d" % h, [P, Z], F32) for h in range(2)]
        diff = [sb("diff%d" % h, [P, Z], F32) for h in range(2)]
        dist = [sb("dist%d" % h, [P, Z], F32) for h in range(2)]
        res = [sb("res%d" % h, [P, Z], F32) for h in range(2)]
        for h in range(2):
            for a, (cols, part) in enumerate(halves(art_sb)):
                nc.vector.tensor_tensor(fr[h][:, cols], sc_ps[h, a][:], fade[:, cols], ALU.mult)
            for a, (cols, part) in enumerate(halves(dup_sb)):
                fetch("scalar" if a == 0 else "vector", twin[h][:, cols], fr[h][:], part)
            for cols, part in halves(dup_sb):
                nc.scalar.activation(tfr[h][:, cols], fr[h][:, cols], ACT.Tanh)
        for h in range(2):
            for cols, part in halves(dup_sb):
                nc.vector.tensor_tensor(diff[h][:, cols], fr[h][:, cols], twin[h][:, cols], ALU.subtract)
            for cols, part in halves(dup_sb):
                nc.scalar.activation(dist[h][:, cols], diff[h][:, cols], ACT.Abs, scale=0.6)
            for cols, part in halves(dup_sb):
                nc.vector.tensor_tensor(res[h][:, cols], dist[h][:, cols], tfr[h][:, cols], ALU.add)
                nc.sync.dma_start(out[P * h : P * (h + 1), cols], res[h][:, cols])
